import numpy as np
import ml_dtypes


def mxq(x, axis, fmt="e4m3"):
    dtype, down = {"e4m3": (ml_dtypes.float8_e4m3fn, 7), "e5m2": (ml_dtypes.float8_e5m2, 14)}[fmt]
    v = np.moveaxis(np.asarray(x, np.float32).astype(ml_dtypes.bfloat16).astype(np.float64), axis, -1)
    blocks = v.reshape(v.shape[:-1] + (-1, 32))
    amax = np.abs(blocks).max(-1, keepdims=True)
    byte = np.maximum(np.where(amax > 0, np.frexp(amax)[1] - 1 + 127, 0) - down, 1)
    scale = np.exp2(byte - 127.0)
    codes = (blocks / scale).astype(np.float32).astype(dtype).astype(np.float64)
    return np.moveaxis((codes * scale).reshape(v.shape), -1, axis)


WIDE = False


def mx_kscale(k):
    if not WIDE:
        return np.ones(k)
    levels = np.array([10, -10, 5, -5, 0])
    if k % 512:
        return np.exp2(np.random.permutation(np.resize(levels, k // 32))).repeat(32)
    a = np.empty((k // 512, 16))
    for p in range(k // 512):
        a[p, :8] = np.random.permutation(np.resize(levels, 8))
        for g in range(8):
            far = levels[np.abs(levels - a[p, g]) >= 10]
            a[p, g + 8] = far[np.random.randint(len(far))]
    return np.exp2(a.ravel()).repeat(32)


def f64(x):
    return np.asarray(x).astype(np.float64)


def striped(idx):
    return np.tile(idx.reshape(-1, 16).T, (8, 1)).astype(np.uint16)


def unstriped(offs):
    return offs[:16].T.reshape(-1).astype(np.int64)


def striped8(idx):
    return np.concatenate([x.reshape(-1, 16).T for x in idx]).astype(np.uint16)


def runs(offs, k):
    lists = np.stack([offs[16 * r : 16 * r + 16].T.reshape(-1) for r in range(8)]).astype(np.int64)
    return lists[np.arange(k) % 512 // 64]


def pack_weight(w):
    k, n = w.shape
    w = f64(np.asarray(w, np.float32).astype(ml_dtypes.bfloat16)).reshape(k // 32, 32, n)
    amax = np.abs(w).max(1)
    byte = np.clip(np.where(amax > 0, np.frexp(amax)[1] - 1 + 127 - 7, 1), 1, 254)
    scaled = (w * np.exp2(127.0 - byte)[:, None, :]).reshape(k, n).astype(np.float32)
    words = np.ascontiguousarray(scaled.reshape(k // 512, 128, 4, n).transpose(0, 1, 3, 2)).astype(ml_dtypes.float8_e4m3fn).view(np.uint8)
    return words, np.ascontiguousarray(byte.astype(np.uint8).reshape(k // 512, 16, n))


def unpack_weight(words, scales):
    g, p, n, _ = words.shape
    vals = np.ascontiguousarray(words).view(ml_dtypes.float8_e4m3fn).astype(np.float64) * np.repeat(np.exp2(scales.astype(np.float64) - 127.0), 8, axis=1)[..., None]
    return vals.transpose(0, 1, 3, 2).reshape(g * 512, n)


E2M1 = np.array([0.0, 0.5, 1.0, 1.5, 2.0, 3.0, 4.0, 6.0, -0.0, -0.5, -1.0, -1.5, -2.0, -3.0, -4.0, -6.0])


def pack_fp4(w):
    k, n = w.shape
    w = f64(np.asarray(w, np.float32).astype(ml_dtypes.bfloat16)).reshape(k // 32, 32, n)
    amax = np.abs(w).max(1)
    mant, ex = np.frexp(amax / 6.0)
    byte = np.clip(np.where(amax > 0, np.where(mant > 0.5, ex, ex - 1) + 127, 1), 1, 254)
    scaled = (w * np.exp2(127.0 - byte)[:, None, :]).reshape(k, n).astype(np.float32)
    c = np.ascontiguousarray(scaled.reshape(k // 512, 128, 4, n).transpose(0, 1, 3, 2)).astype(ml_dtypes.float4_e2m1fn).view(np.uint8) & 0xF
    words = (c[..., 0::2] | (c[..., 1::2] << 4)).reshape(k // 512, 128, 2 * n)
    return np.ascontiguousarray(words), np.ascontiguousarray(byte.astype(np.uint8).reshape(k // 512, 16, n))


def unpack_fp4(words, scales):
    g, _, n = scales.shape
    words = np.ascontiguousarray(words).reshape(g, 128, n, 2)
    nib = np.empty((g, 128, n, 4), np.uint8)
    nib[..., 0::2] = words & 0xF
    nib[..., 1::2] = words >> 4
    vals = E2M1[nib] * np.repeat(np.exp2(scales.astype(np.float64) - 127.0), 8, axis=1)[..., None]
    return vals.transpose(0, 1, 3, 2).reshape(g * 512, n)


def planes(y):
    n, m = y.shape
    v = y.astype(np.float32).astype(ml_dtypes.bfloat16).astype(np.float64).reshape(n // 32, 32, m)
    top = np.abs(v).max(1)
    byte = np.clip(np.where(top > 0, np.frexp(top)[1] - 1 + 127 - 7, 1), 1, 254)
    codes = (v * np.exp2(127.0 - byte)[:, None, :]).reshape(n, m).astype(np.float32).astype(ml_dtypes.float8_e4m3fn).view(np.uint8)
    words = codes.reshape(n // 512, 128, 4, m).transpose(0, 1, 3, 2)
    return np.ascontiguousarray(words), np.ascontiguousarray(byte.astype(np.uint8).reshape(n // 512, 16, m))


K, T, S, N, H = 512, 2048, 512, 512, 512


def setup_inputs():
    n = np.random.standard_normal
    s = mx_kscale(K)[:, None]
    u = mx_kscale(H)
    packed_xT = pack_weight(n((K, T)) * s)
    packed_w1 = pack_fp4(n((K, H)) / np.sqrt(K) / s)
    packed_w2 = pack_fp4(n((H, N)) / np.sqrt(H) / u[:, None])
    return {
        "x_words": packed_xT[0],
        "x_scales": packed_xT[1],
        "w1_words": packed_w1[0],
        "w1_scales": packed_w1[1],
        "gn": (np.random.uniform(0.5, 1.5, (H, 1)) * u[:, None]).astype(np.float32),
        "w2_words": packed_w2[0],
        "w2_scales": packed_w2[1],
        "offs": striped(np.random.permutation(T)[:S]),
        "n1": striped8(np.stack([np.random.permutation(S) for _ in range(8)])),
        "n2": striped8(np.stack([np.random.permutation(S) for _ in range(8)])),
        "n3": striped8(np.stack([np.random.permutation(S) for _ in range(8)])),
        "n4": striped8(np.stack([np.random.permutation(S) for _ in range(8)])),
    }


def reference(x_words, x_scales, w1_words, w1_scales, gn, w2_words, w2_scales, offs, n1, n2, n3, n4):
    xq = unpack_weight(x_words, x_scales)[:, unstriped(offs)]
    y = unpack_fp4(w1_words, w1_scales).T @ xq
    z = f64(gn) * (y / (np.abs(y[np.arange(H)[:, None], runs(n1, H)]) + 0.5))
    h = unpack_fp4(w2_words, w2_scales).T @ mxq(z, 0, "e4m3")
    out_0 = y * (h[np.arange(N)[:, None], runs(n2, N)] - h) + 0.5 * ((y[np.arange(H)[:, None], runs(n4, H)]) * (h[np.arange(N)[:, None], runs(n3, N)] - h))
    return (out_0,) + planes(out_0)

@@ -1,0 +1,221 @@
+from contextlib import ExitStack
+
+import concourse.mybir as mybir
+
+F32 = mybir.dt.float32
+BF16 = mybir.dt.bfloat16
+I32 = mybir.dt.int32
+U32 = mybir.dt.uint32
+U16 = mybir.dt.uint16
+U8 = mybir.dt.uint8
+FP8X4 = mybir.dt.float8_e4m3fn_x4
+FP4X4 = mybir.dt.float4_e2m1fn_x4
+ALU = mybir.AluOpType
+ACT = mybir.ActivationFunctionType
+
+P = 128
+PACK = 4
+T = 2048
+S = 512
+FLOPS = 2 * 2 * 512 * 512 * 512
+Z_CHUNKS = ((0, 256), (256, 512))
+OUT_CHUNKS = ((0, 256), (256, 384), (384, 512))
+EARLY_TILES = 1
+
+
+def load_scale_rows(queues, plane, rows):
+    for q, queue in enumerate(queues):
+        queue.dma_start(out=plane[32 * q : 32 * q + 4, :].bitcast(I32), in_=rows[4 * q : 4 * q + 4, :].bitcast(I32))
+
+
+def interleave(copy, packed, planes):
+    copy(
+        out=packed.rearrange("p (c i t) -> p c t i", i=4, t=PACK),
+        in_=planes.rearrange("p t (c i) -> p c t i", i=4),
+    )
+
+
+def tile_picked_skipflowbnorm_none_po_kernel(
+    tc, x_words, x_scales, w1_words, w1_scales, gn, w2_words, w2_scales, offs, n1, n2, n3, n4, out_0, out_1, out_2
+):
+    nc = tc.nc
+    with ExitStack() as ctx:
+        lists = ctx.enter_context(tc.tile_pool(name="lists", bufs=1))
+        keep = ctx.enter_context(tc.tile_pool(name="keep", bufs=1))
+        raw = ctx.enter_context(tc.tile_pool(name="raw", bufs=1))
+        work = ctx.enter_context(tc.tile_pool(name="work", bufs=3))
+        psum = ctx.enter_context(tc.psum_pool(name="psum", bufs=8))
+
+        def entries(lst, lo, hi):
+            return lst[:, lo // 16 : hi // 16]
+
+        x_scale_table = keep.tile([P, T], U8, align_bytes=64)
+        nc.gpsimd.memset(x_scale_table[:].bitcast(I32), 0)
+        w1_scale_raw = raw.tile([P, 512], U8, tag="w1_scale_raw")
+        nc.gpsimd.memset(w1_scale_raw[:].bitcast(I32), 0)
+        half = keep.tile([P, 1], F32)
+        nc.vector.memset(half[:], 0.5)
+
+        offs_sb = lists.tile([P, S // 16], U16)
+        nc.sync.dma_start(offs_sb[:], offs)
+        w1_raw = raw.tile([P, 1024], U8, tag="w_raw")
+        nc.sync.dma_start(out=w1_raw[:].bitcast(I32), in_=w1_words[0].bitcast(I32))
+        x_word_table = keep.tile([P, T], U32, align_bytes=64)
+        nc.sync.dma_start(
+            out=x_word_table[:].bitcast(I32), in_=x_words[0].rearrange("p c r -> p (c r)").bitcast(I32)
+        )
+        load_scale_rows([nc.scalar] * 4, x_scale_table, x_scales[0])
+        load_scale_rows([nc.sync] * 3 + [nc.gpsimd], w1_scale_raw, w1_scales[0])
+        gain = keep.tile([P, PACK], F32)
+        nc.gpsimd.dma_start(out=gain[:], in_=gn.rearrange("(p t) o -> p (t o)", t=PACK))
+        table_warm = keep.tile([P, 1], F32)
+        nc.scalar.activation(out=table_warm[:], in_=half[:], func=ACT.Abs_reciprocal_sqrt, bias=half[:])
+
+        def deal(words_raw, scales_raw, name):
+            words = keep.tile([P, 1024], U8, name=name + "_words", align_bytes=64)
+            scales = keep.tile([P, 512], U8, name=name + "_scales", align_bytes=64)
+            nc.vector.tensor_copy(
+                out=words[:].bitcast(U16).rearrange("p (t m) -> p t m", t=PACK),
+                in_=words_raw[:].bitcast(U16).rearrange("p (m t) -> p t m", t=PACK),
+            )
+            nc.vector.tensor_copy(
+                out=scales[:].rearrange("p (t m) -> p t m", t=PACK),
+                in_=scales_raw[:].rearrange("p (m t) -> p t m", t=PACK),
+            )
+            return words, scales
+
+        def product(acc, weights, t, codes, scales):
+            nc.tensor.matmul_mx(
+                out=acc,
+                lhsT=weights[0][:, 256 * t : 256 * (t + 1)].bitcast(FP4X4),
+                lhsT_scale=weights[1][:, 128 * t : 128 * (t + 1)],
+                rhs=codes.bitcast(FP8X4),
+                rhs_scale=scales,
+                start=True,
+                stop=True,
+            )
+
+        w1 = deal(w1_raw, w1_scale_raw, "w1")
+        x_scale = keep.tile([P, S], U8, align_bytes=64)
+        nc.vector.tensor_copy(out=x_scale[:], in_=x_scale_table[:].indirect(offs_sb[:]))
+        x_code = keep.tile([P, S], U32, align_bytes=64)
+        for lo, hi in Z_CHUNKS:
+            nc.vector.tensor_copy(out=x_code[:, lo:hi], in_=x_word_table[:].indirect(entries(offs_sb, lo, hi)))
+
+        w2_raw = raw.tile([P, 1024], U8, tag="w_raw")
+        nc.sync.dma_start(out=w2_raw[:].bitcast(I32), in_=w2_words[0].bitcast(I32))
+        w2_scale_raw = raw.tile([P, 512], U8, tag="w2_scale_raw")
+        nc.gpsimd.memset(w2_scale_raw[:].bitcast(I32), 0)
+        load_scale_rows([nc.sync] * 4, w2_scale_raw, w2_scales[0])
+        n1_sb = lists.tile([P, S // 16], U16)
+        nc.sync.dma_start(n1_sb[:], n1)
+        n4_sb = lists.tile([P, S // 16], U16)
+        nc.sync.dma_start(n4_sb[:], n4)
+        n2_sb = lists.tile([P, S // 16], U16)
+        nc.sync.dma_start(n2_sb[:], n2)
+        n3_sb = lists.tile([P, S // 16], U16)
+        nc.sync.dma_start(n3_sb[:], n3)
+        w2 = deal(w2_raw, w2_scale_raw, "w2")
+
+        y = [keep.tile([P, S], F32, name=f"y{t}") for t in range(PACK)]
+        z = [keep.tile([P, PACK, hi - lo], F32, name=f"z{lo}") for lo, hi in Z_CHUNKS]
+        factor = []
+        for t in range(PACK):
+            size = work.tile([P, S], F32)
+            root = work.tile([P, S], F32)
+            spans = Z_CHUNKS if t == 0 else ((0, S),)
+            accs = []
+            for lo, hi in spans:
+                acc = psum.tile([P, hi - lo], F32, tag="acc")
+                product(acc[:], w1, t, x_code[:, lo:hi], x_scale[:, lo:hi])
+                nc.scalar.activation(out=size[:, lo:hi], in_=acc[:], func=ACT.Abs)
+                nc.scalar.activation(
+                    out=root[:, lo:hi], in_=size[:, lo:hi], func=ACT.Abs_reciprocal_sqrt, bias=half[:]
+                )
+                accs.append(acc)
+            for (lo, hi), acc in zip(spans, accs):
+                nc.scalar.copy(out=y[t][:, lo:hi], in_=acc[:])
+            factor.append(keep.tile([P, S], F32, name=f"factor{t}"))
+            nc.vector.scalar_tensor_tensor(
+                out=factor[t][:], in0=root[:], scalar=gain[:, t : t + 1], in1=root[:], op0=ALU.mult, op1=ALU.mult
+            )
+            for u, c in ((t - 1, 1), (t, 0), (t, 1)):
+                if u >= 0 and (u != t or c == 0 or t == PACK - 1):
+                    lo, hi = Z_CHUNKS[c]
+                    nc.vector.tensor_tensor(
+                        z[c][:, u, :], factor[u][:].indirect(entries(n1_sb, lo, hi)), y[u][:, lo:hi], ALU.mult
+                    )
+
+        h = [keep.tile([P, S], F32, name=f"h{t}") for t in range(PACK)]
+        h_here = [keep.tile([P, S], F32, name=f"h_here{t}") for t in range(PACK)]
+        z_packed = []
+        for c, ((lo, hi), z_part) in enumerate(zip(Z_CHUNKS, z)):
+            packed = keep.tile([P, PACK * (hi - lo)], BF16, name=f"z_packed{lo}", align_bytes=64)
+            interleave(nc.scalar.copy if c == 0 else nc.vector.tensor_copy, packed[:], z_part[:])
+            z_packed.append(packed)
+        for (lo, hi), packed in zip(Z_CHUNKS, z_packed):
+            z_code = keep.tile([P, hi - lo], U32, name=f"z_code{lo}", align_bytes=64)
+            z_scale = keep.tile([P, hi - lo], U8, name=f"z_scale{lo}", align_bytes=64)
+            nc.vector.quantize_mx(out=z_code[:].bitcast(FP8X4), scales=z_scale[:], in_=packed[:])
+            for t in range(PACK):
+                acc = psum.tile([P, hi - lo], F32, tag="acc")
+                product(acc[:], w2, t, z_code[:], z_scale[:])
+                nc.scalar.copy(out=h[t][:, lo:hi], in_=acc[:])
+                nc.scalar.copy(out=h_here[t][:, lo:hi], in_=acc[:])
+
+        y_far = [keep.tile([P, S], F32, name=f"y_far{t}") for t in range(EARLY_TILES)]
+        for t in range(EARLY_TILES):
+            for lo, hi in Z_CHUNKS:
+                nc.vector.tensor_copy(out=y_far[t][:, lo:hi], in_=y[t][:].indirect(entries(n4_sb, lo, hi)))
+
+        out_code = keep.tile([P, S], U32, align_bytes=64)
+        out_scale = keep.tile([P, S], U8, align_bytes=64)
+        out_rows = out_0.rearrange("(p t) j -> p t j", t=PACK)
+        out_words = out_1[0].rearrange("p c r -> p (c r)").bitcast(I32)
+
+        def add_up(lo, hi, near, far):
+            res = keep.tile([P, PACK, hi - lo], F32, name=f"res{lo}")
+            nc.vector.scalar_tensor_tensor(
+                out=res[:], in0=far[:], scalar=0.5, in1=near[:], op0=ALU.mult, op1=ALU.add
+            )
+            nc.sync.dma_start(out=out_rows[:, :, lo:hi], in_=res[:])
+            packed = keep.tile([P, PACK * (hi - lo)], BF16, name=f"out_packed{lo}", align_bytes=64)
+            interleave(nc.vector.tensor_copy if hi == S else nc.scalar.copy, packed[:], res[:])
+            return packed
+
+        def hand_on(lo, hi, packed):
+            nc.vector.quantize_mx(out=out_code[:, lo:hi].bitcast(FP8X4), scales=out_scale[:, lo:hi], in_=packed[:])
+            nc.sync.dma_start(out=out_words[:, lo:hi], in_=out_code[:, lo:hi].bitcast(I32))
+
+        last = None
+        for lo, hi in OUT_CHUNKS:
+            n = hi - lo
+            near = keep.tile([P, PACK, n], F32, name=f"near{lo}")
+            far = keep.tile([P, PACK, n], F32, name=f"far{lo}")
+            for t in range(PACK):
+                step2 = work.tile([P, n], F32)
+                nc.vector.tensor_tensor(
+                    step2[:], h[t][:].indirect(entries(n2_sb, lo, hi)), h_here[t][:, lo:hi], ALU.subtract
+                )
+                if last is not None and t == 0:
+                    last_packed = add_up(*last)
+                step3 = work.tile([P, n], F32)
+                nc.vector.tensor_tensor(
+                    step3[:], h[t][:].indirect(entries(n3_sb, lo, hi)), h_here[t][:, lo:hi], ALU.subtract
+                )
+                nc.vector.tensor_tensor(near[:, t, :], y[t][:, lo:hi], step2[:], ALU.mult)
+                if t < EARLY_TILES:
+                    nc.vector.tensor_tensor(far[:, t, :], y_far[t][:, lo:hi], step3[:], ALU.mult)
+                else:
+                    nc.vector.tensor_tensor(
+                        far[:, t, :], y[t][:].indirect(entries(n4_sb, lo, hi)), step3[:], ALU.mult
+                    )
+                if last is not None and t == 2:
+                    hand_on(last[0], last[1], last_packed)
+            last = (lo, hi, near, far)
+        hand_on(last[0], last[1], add_up(*last))
+        for q in range(4):
+            queue = nc.scalar if q % 2 == 0 else nc.sync
+            queue.dma_start(
+                out=out_2[0][4 * q : 4 * q + 4, :].bitcast(I32), in_=out_scale[32 * q : 32 * q + 4, :].bitcast(I32)
+            )

@@ -1,6 +1,7 @@
 from contextlib import ExitStack
 
 import concourse.mybir as mybir
+from concourse.masks import make_identity
 
 F32 = mybir.dt.float32
 BF16 = mybir.dt.bfloat16
@@ -18,8 +19,9 @@ PACK = 4
 T = 2048
 S = 512
 FLOPS = 2 * 2 * 512 * 512 * 512
-Z_CHUNKS = ((0, 256), (256, 512))
-OUT_CHUNKS = ((0, 256), (256, 384), (384, 512))
+HALVES = ((0, 256), (256, 512))
+BULK = 384
+SCALAR_SQUARES = ()
 EARLY_TILES = 1
 
 
@@ -35,6 +37,10 @@ def interleave(copy, packed, planes):
     )
 
 
+def entries(lst, lo, hi):
+    return lst[:, lo // 16 : hi // 16]
+
+
 def tile_picked_skipflowbnorm_none_po_kernel(
     tc, x_words, x_scales, w1_words, w1_scales, gn, w2_words, w2_scales, offs, n1, n2, n3, n4, out_0, out_1, out_2
 ):
@@ -46,15 +52,18 @@ def tile_picked_skipflowbnorm_none_po_kernel(
         work = ctx.enter_context(tc.tile_pool(name="work", bufs=3))
         psum = ctx.enter_context(tc.psum_pool(name="psum", bufs=8))
 
-        def entries(lst, lo, hi):
-            return lst[:, lo // 16 : hi // 16]
-
-        x_scale_table = keep.tile([P, T], U8, align_bytes=64)
-        nc.gpsimd.memset(x_scale_table[:].bitcast(I32), 0)
-        w1_scale_raw = raw.tile([P, 512], U8, tag="w1_scale_raw")
+        consts = keep.tile([P, 16], F32)
+        nc.gpsimd.memset(consts[:], 0.5)
+        half = consts[:, 8:9]
+        gain = consts[:, 0:PACK]
+        table_warm = keep.tile([P, 1], F32)
+        nc.scalar.activation(out=table_warm[:], in_=half, func=ACT.Abs_reciprocal_sqrt, bias=half)
+        w1_scale_raw = raw.tile([P, 512], U8, tag="w1_scale_raw", align_bytes=64)
         nc.gpsimd.memset(w1_scale_raw[:].bitcast(I32), 0)
-        half = keep.tile([P, 1], F32)
-        nc.vector.memset(half[:], 0.5)
+        x_scale_table = keep.tile([P, T], U8, align_bytes=64)
+        nc.vector.memset(x_scale_table[:].bitcast(I32), 0)
+        w2_scale_raw = raw.tile([P, 512], U8, tag="w2_scale_raw")
+        nc.vector.memset(w2_scale_raw[:].bitcast(I32), 0)
 
         offs_sb = lists.tile([P, S // 16], U16)
         nc.sync.dma_start(offs_sb[:], offs)
@@ -65,20 +74,17 @@ def tile_picked_skipflowbnorm_none_po_kernel(
             out=x_word_table[:].bitcast(I32), in_=x_words[0].rearrange("p c r -> p (c r)").bitcast(I32)
         )
         load_scale_rows([nc.scalar] * 4, x_scale_table, x_scales[0])
-        load_scale_rows([nc.sync] * 3 + [nc.gpsimd], w1_scale_raw, w1_scales[0])
-        gain = keep.tile([P, PACK], F32)
-        nc.gpsimd.dma_start(out=gain[:], in_=gn.rearrange("(p t) o -> p (t o)", t=PACK))
-        table_warm = keep.tile([P, 1], F32)
-        nc.scalar.activation(out=table_warm[:], in_=half[:], func=ACT.Abs_reciprocal_sqrt, bias=half[:])
+        load_scale_rows([nc.scalar] * 2 + [nc.gpsimd] * 2, w1_scale_raw, w1_scales[0])
+        nc.gpsimd.dma_start(out=gain, in_=gn.rearrange("(p t) o -> p (t o)", t=PACK))
 
-        def deal(words_raw, scales_raw, name):
-            words = keep.tile([P, 1024], U8, name=name + "_words", align_bytes=64)
+        def deal(words_raw, scales_raw, name, words_tag, scale_engine):
+            words = raw.tile([P, 1024], U8, name=name + "_words", tag=words_tag, align_bytes=64)
             scales = keep.tile([P, 512], U8, name=name + "_scales", align_bytes=64)
             nc.vector.tensor_copy(
                 out=words[:].bitcast(U16).rearrange("p (t m) -> p t m", t=PACK),
                 in_=words_raw[:].bitcast(U16).rearrange("p (m t) -> p t m", t=PACK),
             )
-            nc.vector.tensor_copy(
+            scale_engine.tensor_copy(
                 out=scales[:].rearrange("p (t m) -> p t m", t=PACK),
                 in_=scales_raw[:].rearrange("p (m t) -> p t m", t=PACK),
             )
@@ -95,77 +101,89 @@ def tile_picked_skipflowbnorm_none_po_kernel(
                 stop=True,
             )
 
-        w1 = deal(w1_raw, w1_scale_raw, "w1")
+        w1 = deal(w1_raw, w1_scale_raw, "w1", "w1_words", nc.vector)
         x_scale = keep.tile([P, S], U8, align_bytes=64)
         nc.vector.tensor_copy(out=x_scale[:], in_=x_scale_table[:].indirect(offs_sb[:]))
         x_code = keep.tile([P, S], U32, align_bytes=64)
-        for lo, hi in Z_CHUNKS:
+        for lo, hi in HALVES:
             nc.vector.tensor_copy(out=x_code[:, lo:hi], in_=x_word_table[:].indirect(entries(offs_sb, lo, hi)))
 
-        w2_raw = raw.tile([P, 1024], U8, tag="w_raw")
-        nc.sync.dma_start(out=w2_raw[:].bitcast(I32), in_=w2_words[0].bitcast(I32))
-        w2_scale_raw = raw.tile([P, 512], U8, tag="w2_scale_raw")
-        nc.gpsimd.memset(w2_scale_raw[:].bitcast(I32), 0)
-        load_scale_rows([nc.sync] * 4, w2_scale_raw, w2_scales[0])
         n1_sb = lists.tile([P, S // 16], U16)
         nc.sync.dma_start(n1_sb[:], n1)
+        load_scale_rows([nc.scalar] * 4, w2_scale_raw, w2_scales[0])
+        w2_raw = raw.tile([P, 1024], U8, tag="w_raw")
+        nc.scalar.dma_start(out=w2_raw[:].bitcast(I32), in_=w2_words[0].bitcast(I32))
         n4_sb = lists.tile([P, S // 16], U16)
         nc.sync.dma_start(n4_sb[:], n4)
         n2_sb = lists.tile([P, S // 16], U16)
         nc.sync.dma_start(n2_sb[:], n2)
         n3_sb = lists.tile([P, S // 16], U16)
         nc.sync.dma_start(n3_sb[:], n3)
-        w2 = deal(w2_raw, w2_scale_raw, "w2")
+        w2 = deal(w2_raw, w2_scale_raw, "w2", "w1_scale_raw", nc.gpsimd)
 
+        identity = keep.tile([P, P], F32)
+        make_identity(nc, identity[:])
         y = [keep.tile([P, S], F32, name=f"y{t}") for t in range(PACK)]
-        z = [keep.tile([P, PACK, hi - lo], F32, name=f"z{lo}") for lo, hi in Z_CHUNKS]
-        factor = []
+        z = [keep.tile([P, PACK, hi - lo], F32, name=f"z{lo}") for lo, hi in HALVES]
+        h_wide = [keep.tile([P, 2 * S], F32, name=f"h_wide{t}") for t in range(PACK)]
+        h = [keep.tile([P, S], F32, name=f"h{t}") for t in range(PACK)]
+        factor = [keep.tile([P, S], F32, name=f"factor{t}") for t in range(PACK)]
+
+        scaled = [keep.tile([P, S], F32, name=f"scaled{t}") if t in SCALAR_SQUARES else y[t] for t in range(PACK)]
+        held = []
+
+        def normalise(t, c):
+            lo, hi = HALVES[c]
+            nc.vector.tensor_tensor(
+                z[c][:, t, :], factor[t][:].indirect(entries(n1_sb, lo, hi)), scaled[t][:, lo:hi], ALU.mult
+            )
+
         for t in range(PACK):
-            size = work.tile([P, S], F32)
+            size = h_wide[t][:, S:]
             root = work.tile([P, S], F32)
-            spans = Z_CHUNKS if t == 0 else ((0, S),)
+            spans = HALVES if t == 0 else ((0, S),)
             accs = []
             for lo, hi in spans:
                 acc = psum.tile([P, hi - lo], F32, tag="acc")
                 product(acc[:], w1, t, x_code[:, lo:hi], x_scale[:, lo:hi])
                 nc.scalar.activation(out=size[:, lo:hi], in_=acc[:], func=ACT.Abs)
-                nc.scalar.activation(
-                    out=root[:, lo:hi], in_=size[:, lo:hi], func=ACT.Abs_reciprocal_sqrt, bias=half[:]
-                )
+                nc.scalar.activation(out=root[:, lo:hi], in_=size[:, lo:hi], func=ACT.Abs_reciprocal_sqrt, bias=half)
                 accs.append(acc)
-            for (lo, hi), acc in zip(spans, accs):
-                nc.scalar.copy(out=y[t][:, lo:hi], in_=acc[:])
-            factor.append(keep.tile([P, S], F32, name=f"factor{t}"))
-            nc.vector.scalar_tensor_tensor(
-                out=factor[t][:], in0=root[:], scalar=gain[:, t : t + 1], in1=root[:], op0=ALU.mult, op1=ALU.mult
-            )
-            for u, c in ((t - 1, 1), (t, 0), (t, 1)):
-                if u >= 0 and (u != t or c == 0 or t == PACK - 1):
-                    lo, hi = Z_CHUNKS[c]
-                    nc.vector.tensor_tensor(
-                        z[c][:, u, :], factor[u][:].indirect(entries(n1_sb, lo, hi)), y[u][:, lo:hi], ALU.mult
-                    )
+            if t in SCALAR_SQUARES:
+                nc.scalar.activation(out=scaled[t][:], in_=accs[0][:], func=ACT.Copy, scale=gain[:, t : t + 1])
+                nc.scalar.activation(out=factor[t][:], in_=root[:], func=ACT.Square)
+                held.append((t, accs[0]))
+            else:
+                for (lo, hi), acc in zip(spans, accs):
+                    nc.scalar.copy(out=y[t][:, lo:hi], in_=acc[:])
+                nc.vector.scalar_tensor_tensor(
+                    out=factor[t][:], in0=root[:], scalar=gain[:, t : t + 1], in1=root[:], op0=ALU.mult, op1=ALU.mult
+                )
+            if t in (1, 2):
+                normalise(t - 1, 1)
+            normalise(t, 0)
+        normalise(2, 1)
+        normalise(3, 1)
 
-        h = [keep.tile([P, S], F32, name=f"h{t}") for t in range(PACK)]
-        h_here = [keep.tile([P, S], F32, name=f"h_here{t}") for t in range(PACK)]
-        z_packed = []
-        for c, ((lo, hi), z_part) in enumerate(zip(Z_CHUNKS, z)):
-            packed = keep.tile([P, PACK * (hi - lo)], BF16, name=f"z_packed{lo}", align_bytes=64)
-            interleave(nc.scalar.copy if c == 0 else nc.vector.tensor_copy, packed[:], z_part[:])
-            z_packed.append(packed)
-        for (lo, hi), packed in zip(Z_CHUNKS, z_packed):
-            z_code = keep.tile([P, hi - lo], U32, name=f"z_code{lo}", align_bytes=64)
-            z_scale = keep.tile([P, hi - lo], U8, name=f"z_scale{lo}", align_bytes=64)
-            nc.vector.quantize_mx(out=z_code[:].bitcast(FP8X4), scales=z_scale[:], in_=packed[:])
-            for t in range(PACK):
+        z_code = keep.tile([P, S], U32, align_bytes=64)
+        z_scale = keep.tile([P, S], U8, align_bytes=64)
+        for c, (lo, hi) in enumerate(HALVES):
+            packed = raw.tile([P, PACK * (hi - lo)], BF16, tag=f"z_packed{c}", align_bytes=64)
+            interleave(nc.scalar.copy if c == 0 else nc.vector.tensor_copy, packed[:], z[c][:])
+            nc.vector.quantize_mx(out=z_code[:, lo:hi].bitcast(FP8X4), scales=z_scale[:, lo:hi], in_=packed[:])
+        for t, acc in held:
+            nc.scalar.copy(out=y[t][:], in_=acc[:])
+        for t in range(PACK):
+            for lo, hi in HALVES:
                 acc = psum.tile([P, hi - lo], F32, tag="acc")
-                product(acc[:], w2, t, z_code[:], z_scale[:])
+                product(acc[:], w2, t, z_code[:, lo:hi], z_scale[:, lo:hi])
+                nc.scalar.copy(out=h_wide[t][:, lo:hi], in_=acc[:])
                 nc.scalar.copy(out=h[t][:, lo:hi], in_=acc[:])
-                nc.scalar.copy(out=h_here[t][:, lo:hi], in_=acc[:])
 
-        y_far = [keep.tile([P, S], F32, name=f"y_far{t}") for t in range(EARLY_TILES)]
+        spans = ((0, BULK), (BULK, S))
+        y_far = [raw.tile([P, S], F32, name=f"y_far{t}", tag=f"z_packed{1 - t}", align_bytes=64) for t in range(EARLY_TILES)]
         for t in range(EARLY_TILES):
-            for lo, hi in Z_CHUNKS:
+            for lo, hi in spans:
                 nc.vector.tensor_copy(out=y_far[t][:, lo:hi], in_=y[t][:].indirect(entries(n4_sb, lo, hi)))
 
         out_code = keep.tile([P, S], U32, align_bytes=64)
@@ -173,47 +191,59 @@ def tile_picked_skipflowbnorm_none_po_kernel(
         out_rows = out_0.rearrange("(p t) j -> p t j", t=PACK)
         out_words = out_1[0].rearrange("p c r -> p (c r)").bitcast(I32)
 
-        def add_up(lo, hi, near, far):
-            res = keep.tile([P, PACK, hi - lo], F32, name=f"res{lo}")
+        def terms(t, lo, hi, window, here, near, far, near_gain):
+            step2 = work.tile([P, hi - lo], F32)
+            nc.vector.tensor_tensor(step2[:], window[:].indirect(entries(n2_sb, lo, hi)), here[:, lo:hi], ALU.subtract)
+            step3 = work.tile([P, hi - lo], F32)
+            nc.vector.tensor_tensor(step3[:], window[:].indirect(entries(n3_sb, lo, hi)), here[:, lo:hi], ALU.subtract)
             nc.vector.scalar_tensor_tensor(
-                out=res[:], in0=far[:], scalar=0.5, in1=near[:], op0=ALU.mult, op1=ALU.add
+                out=near, in0=y[t][:, lo:hi], scalar=near_gain, in1=step2[:], op0=ALU.mult, op1=ALU.mult
             )
-            nc.sync.dma_start(out=out_rows[:, :, lo:hi], in_=res[:])
+            if t < EARLY_TILES:
+                nc.vector.tensor_tensor(far, y_far[t][:, lo:hi], step3[:], ALU.mult)
+            else:
+                nc.vector.tensor_tensor(far, y[t][:].indirect(entries(n4_sb, lo, hi)), step3[:], ALU.mult)
+
+        def hand_on(copy, res, lo, hi, first):
             packed = keep.tile([P, PACK * (hi - lo)], BF16, name=f"out_packed{lo}", align_bytes=64)
-            interleave(nc.vector.tensor_copy if hi == S else nc.scalar.copy, packed[:], res[:])
-            return packed
-
-        def hand_on(lo, hi, packed):
+            interleave(copy, packed[:], res[:, :, lo - first : hi - first])
             nc.vector.quantize_mx(out=out_code[:, lo:hi].bitcast(FP8X4), scales=out_scale[:, lo:hi], in_=packed[:])
-            nc.sync.dma_start(out=out_words[:, lo:hi], in_=out_code[:, lo:hi].bitcast(I32))
 
-        last = None
-        for lo, hi in OUT_CHUNKS:
-            n = hi - lo
-            near = keep.tile([P, PACK, n], F32, name=f"near{lo}")
-            far = keep.tile([P, PACK, n], F32, name=f"far{lo}")
-            for t in range(PACK):
-                step2 = work.tile([P, n], F32)
-                nc.vector.tensor_tensor(
-                    step2[:], h[t][:].indirect(entries(n2_sb, lo, hi)), h_here[t][:, lo:hi], ALU.subtract
+        bulk = keep.tile([P, PACK, BULK], F32)
+        for t in range(PACK):
+            near = work.tile([P, BULK], F32)
+            far = work.tile([P, BULK], F32)
+            terms(t, 0, BULK, h_wide[t], h[t], near[:], far[:], 2.0)
+            turned = psum.tile([P, BULK], F32, tag="acc")
+            for b in range(0, BULK, P):
+                nc.tensor.matmul(
+                    turned[:, b : b + P], near[:, b : b + P], identity[:], start=True, stop=False, is_transpose=True
                 )
-                if last is not None and t == 0:
-                    last_packed = add_up(*last)
-                step3 = work.tile([P, n], F32)
-                nc.vector.tensor_tensor(
-                    step3[:], h[t][:].indirect(entries(n3_sb, lo, hi)), h_here[t][:, lo:hi], ALU.subtract
+                nc.tensor.matmul(
+                    turned[:, b : b + P], far[:, b : b + P], identity[:], start=False, stop=True, is_transpose=True
                 )
-                nc.vector.tensor_tensor(near[:, t, :], y[t][:, lo:hi], step2[:], ALU.mult)
-                if t < EARLY_TILES:
-                    nc.vector.tensor_tensor(far[:, t, :], y_far[t][:, lo:hi], step3[:], ALU.mult)
-                else:
-                    nc.vector.tensor_tensor(
-                        far[:, t, :], y[t][:].indirect(entries(n4_sb, lo, hi)), step3[:], ALU.mult
-                    )
-                if last is not None and t == 2:
-                    hand_on(last[0], last[1], last_packed)
-            last = (lo, hi, near, far)
-        hand_on(last[0], last[1], add_up(*last))
+            summed = work.tile([P, BULK], F32)
+            nc.scalar.activation(out=summed[:], in_=turned[:], func=ACT.Copy, scale=0.5)
+            back = psum.tile([P, BULK], F32, tag="acc")
+            for b in range(0, BULK, P):
+                nc.tensor.transpose(back[:, b : b + P], summed[:, b : b + P], identity[:])
+            nc.scalar.copy(out=bulk[:, t, :], in_=back[:])
+            nc.sync.dma_start(out=out_rows[:, t, 0:BULK], in_=bulk[:, t, :])
+
+        near_rest = keep.tile([P, PACK, S - BULK], F32)
+        far_rest = keep.tile([P, PACK, S - BULK], F32)
+        for t in range(PACK):
+            terms(t, BULK, S, h[t], h_wide[t], near_rest[:, t, :], far_rest[:, t, :], 1.0)
+        rest = keep.tile([P, PACK, S - BULK], F32)
+        nc.vector.scalar_tensor_tensor(
+            out=rest[:], in0=far_rest[:], scalar=0.5, in1=near_rest[:], op0=ALU.mult, op1=ALU.add
+        )
+        nc.sync.dma_start(out=out_rows[:, :, BULK:S], in_=rest[:])
+        hand_on(nc.scalar.copy, bulk, 0, 256, 0)
+        hand_on(nc.scalar.copy, bulk, 256, BULK, 0)
+        nc.sync.dma_start(out=out_words[:, 0:BULK], in_=out_code[:, 0:BULK].bitcast(I32))
+        hand_on(nc.vector.tensor_copy, rest, BULK, S, BULK)
+        nc.sync.dma_start(out=out_words[:, BULK:S], in_=out_code[:, BULK:S].bitcast(I32))
         for q in range(4):
             queue = nc.scalar if q % 2 == 0 else nc.sync
             queue.dma_start(

@@ -18,16 +18,24 @@ P = 128
 PACK = 4
 T = 2048
 S = 512
+W = 512
+PER_COLUMN = 16
 FLOPS = 2 * 2 * 512 * 512 * 512
-HALVES = ((0, 256), (256, 512))
+
+HALF = S // 2
+HALVES = ((0, HALF), (HALF, S))
 BULK = 384
-SCALAR_SQUARES = ()
-EARLY_TILES = 1
+PARTS = ((0, BULK), (BULK, S))
+SPLIT_PLANES = 2
+SCALAR_SQUARES_FROM = 2
+LAST = PACK - 1
 
 
-def load_scale_rows(queues, plane, rows):
+def load_scale_rows(queues, scale_tile, rows):
     for q, queue in enumerate(queues):
-        queue.dma_start(out=plane[32 * q : 32 * q + 4, :].bitcast(I32), in_=rows[4 * q : 4 * q + 4, :].bitcast(I32))
+        queue.dma_start(
+            out=scale_tile[32 * q : 32 * q + 4, :].bitcast(I32), in_=rows[4 * q : 4 * q + 4, :].bitcast(I32)
+        )
 
 
 def interleave(copy, packed, planes):
@@ -37,8 +45,8 @@ def interleave(copy, packed, planes):
     )
 
 
-def entries(lst, lo, hi):
-    return lst[:, lo // 16 : hi // 16]
+def entries(list_tile, lo, hi):
+    return list_tile[:, lo // PER_COLUMN : hi // PER_COLUMN]
 
 
 def tile_picked_skipflowbnorm_none_po_kernel(
@@ -48,27 +56,27 @@ def tile_picked_skipflowbnorm_none_po_kernel(
     with ExitStack() as ctx:
         lists = ctx.enter_context(tc.tile_pool(name="lists", bufs=1))
         keep = ctx.enter_context(tc.tile_pool(name="keep", bufs=1))
-        raw = ctx.enter_context(tc.tile_pool(name="raw", bufs=1))
+        reuse = ctx.enter_context(tc.tile_pool(name="reuse", bufs=1))
         work = ctx.enter_context(tc.tile_pool(name="work", bufs=3))
         psum = ctx.enter_context(tc.psum_pool(name="psum", bufs=8))
 
         consts = keep.tile([P, 16], F32)
         nc.gpsimd.memset(consts[:], 0.5)
-        half = consts[:, 8:9]
+        one_half = consts[:, 8:9]
         gain = consts[:, 0:PACK]
         table_warm = keep.tile([P, 1], F32)
-        nc.scalar.activation(out=table_warm[:], in_=half, func=ACT.Abs_reciprocal_sqrt, bias=half)
-        w1_scale_raw = raw.tile([P, 512], U8, tag="w1_scale_raw", align_bytes=64)
+        nc.scalar.activation(out=table_warm[:], in_=one_half, func=ACT.Abs_reciprocal_sqrt, bias=one_half)
+        w1_scale_raw = reuse.tile([P, W], U8, tag="w1_scale_raw", align_bytes=64)
         nc.gpsimd.memset(w1_scale_raw[:].bitcast(I32), 0)
         x_scale_table = keep.tile([P, T], U8, align_bytes=64)
         nc.vector.memset(x_scale_table[:].bitcast(I32), 0)
-        w2_scale_raw = raw.tile([P, 512], U8, tag="w2_scale_raw")
+        w2_scale_raw = reuse.tile([P, W], U8, tag="w2_scale_raw")
         nc.vector.memset(w2_scale_raw[:].bitcast(I32), 0)
 
-        offs_sb = lists.tile([P, S // 16], U16)
+        offs_sb = lists.tile([P, S // PER_COLUMN], U16)
         nc.sync.dma_start(offs_sb[:], offs)
-        w1_raw = raw.tile([P, 1024], U8, tag="w_raw")
-        nc.sync.dma_start(out=w1_raw[:].bitcast(I32), in_=w1_words[0].bitcast(I32))
+        w1_raw = reuse.tile([P, 2 * W], U8, tag="w_raw")
+        nc.scalar.dma_start(out=w1_raw[:].bitcast(I32), in_=w1_words[0].bitcast(I32))
         x_word_table = keep.tile([P, T], U32, align_bytes=64)
         nc.sync.dma_start(
             out=x_word_table[:].bitcast(I32), in_=x_words[0].rearrange("p c r -> p (c r)").bitcast(I32)
@@ -77,9 +85,9 @@ def tile_picked_skipflowbnorm_none_po_kernel(
         load_scale_rows([nc.scalar] * 2 + [nc.gpsimd] * 2, w1_scale_raw, w1_scales[0])
         nc.gpsimd.dma_start(out=gain, in_=gn.rearrange("(p t) o -> p (t o)", t=PACK))
 
-        def deal(words_raw, scales_raw, name, words_tag, scale_engine):
-            words = raw.tile([P, 1024], U8, name=name + "_words", tag=words_tag, align_bytes=64)
-            scales = keep.tile([P, 512], U8, name=name + "_scales", align_bytes=64)
+        def regroup(words_raw, scales_raw, name, words_tag, scale_engine):
+            words = reuse.tile([P, 2 * W], U8, name=name + "_words", tag=words_tag, align_bytes=64)
+            scales = keep.tile([P, W], U8, name=name + "_scales", align_bytes=64)
             nc.vector.tensor_copy(
                 out=words[:].bitcast(U16).rearrange("p (t m) -> p t m", t=PACK),
                 in_=words_raw[:].bitcast(U16).rearrange("p (m t) -> p t m", t=PACK),
@@ -91,100 +99,111 @@ def tile_picked_skipflowbnorm_none_po_kernel(
             return words, scales
 
         def product(acc, weights, t, codes, scales):
+            words, weight_scales = weights
             nc.tensor.matmul_mx(
                 out=acc,
-                lhsT=weights[0][:, 256 * t : 256 * (t + 1)].bitcast(FP4X4),
-                lhsT_scale=weights[1][:, 128 * t : 128 * (t + 1)],
+                lhsT=words[:, 2 * P * t : 2 * P * (t + 1)].bitcast(FP4X4),
+                lhsT_scale=weight_scales[:, P * t : P * (t + 1)],
                 rhs=codes.bitcast(FP8X4),
                 rhs_scale=scales,
                 start=True,
                 stop=True,
             )
 
-        w1 = deal(w1_raw, w1_scale_raw, "w1", "w1_words", nc.vector)
+        w1 = regroup(w1_raw, w1_scale_raw, "w1", "w1_words", nc.vector)
         x_scale = keep.tile([P, S], U8, align_bytes=64)
-        nc.vector.tensor_copy(out=x_scale[:], in_=x_scale_table[:].indirect(offs_sb[:]))
         x_code = keep.tile([P, S], U32, align_bytes=64)
         for lo, hi in HALVES:
+            nc.vector.tensor_copy(out=x_scale[:, lo:hi], in_=x_scale_table[:].indirect(entries(offs_sb, lo, hi)))
             nc.vector.tensor_copy(out=x_code[:, lo:hi], in_=x_word_table[:].indirect(entries(offs_sb, lo, hi)))
 
-        n1_sb = lists.tile([P, S // 16], U16)
+        n1_sb = lists.tile([P, S // PER_COLUMN], U16)
         nc.sync.dma_start(n1_sb[:], n1)
         load_scale_rows([nc.scalar] * 4, w2_scale_raw, w2_scales[0])
-        w2_raw = raw.tile([P, 1024], U8, tag="w_raw")
+        w2_raw = reuse.tile([P, 2 * W], U8, tag="w_raw")
         nc.scalar.dma_start(out=w2_raw[:].bitcast(I32), in_=w2_words[0].bitcast(I32))
-        n4_sb = lists.tile([P, S // 16], U16)
+        n4_sb = lists.tile([P, S // PER_COLUMN], U16)
         nc.sync.dma_start(n4_sb[:], n4)
-        n2_sb = lists.tile([P, S // 16], U16)
+        n2_sb = lists.tile([P, S // PER_COLUMN], U16)
         nc.sync.dma_start(n2_sb[:], n2)
-        n3_sb = lists.tile([P, S // 16], U16)
+        n3_sb = lists.tile([P, S // PER_COLUMN], U16)
         nc.sync.dma_start(n3_sb[:], n3)
-        w2 = deal(w2_raw, w2_scale_raw, "w2", "w1_scale_raw", nc.gpsimd)
+        w2 = regroup(w2_raw, w2_scale_raw, "w2", "w1_scale_raw", nc.gpsimd)
 
         identity = keep.tile([P, P], F32)
         make_identity(nc, identity[:])
-        y = [keep.tile([P, S], F32, name=f"y{t}") for t in range(PACK)]
+
+        y_wide = [keep.tile([P, 2 * S], F32, name=f"y_wide{t}") for t in range(PACK)]
+        y = [wide[:, 0:S] for wide in y_wide]
         z = [keep.tile([P, PACK, hi - lo], F32, name=f"z{lo}") for lo, hi in HALVES]
         h_wide = [keep.tile([P, 2 * S], F32, name=f"h_wide{t}") for t in range(PACK)]
         h = [keep.tile([P, S], F32, name=f"h{t}") for t in range(PACK)]
         factor = [keep.tile([P, S], F32, name=f"factor{t}") for t in range(PACK)]
-
-        scaled = [keep.tile([P, S], F32, name=f"scaled{t}") if t in SCALAR_SQUARES else y[t] for t in range(PACK)]
-        held = []
+        partner = [
+            keep.tile([P, S], F32, name=f"gained_y{t}") if t >= SCALAR_SQUARES_FROM else y[t] for t in range(PACK)
+        ]
+        y_left_in_psum = []
 
         def normalise(t, c):
             lo, hi = HALVES[c]
             nc.vector.tensor_tensor(
-                z[c][:, t, :], factor[t][:].indirect(entries(n1_sb, lo, hi)), scaled[t][:, lo:hi], ALU.mult
+                z[c][:, t, :], factor[t][:].indirect(entries(n1_sb, lo, hi)), partner[t][:, lo:hi], ALU.mult
             )
 
+        def inverse_root(t, lo, hi):
+            acc = psum.tile([P, hi - lo], F32, tag="acc")
+            product(acc[:], w1, t, x_code[:, lo:hi], x_scale[:, lo:hi])
+            size = h_wide[t][:, S + lo : S + hi]
+            nc.scalar.activation(out=size, in_=acc[:], func=ACT.Abs)
+            nc.scalar.activation(
+                out=y_wide[t][:, S + lo : S + hi], in_=size, func=ACT.Abs_reciprocal_sqrt, bias=one_half
+            )
+            return acc
+
+        first_halves = [inverse_root(t, *HALVES[0]) for t in range(SPLIT_PLANES)]
         for t in range(PACK):
-            size = h_wide[t][:, S:]
-            root = work.tile([P, S], F32)
-            spans = HALVES if t == 0 else ((0, S),)
-            accs = []
-            for lo, hi in spans:
-                acc = psum.tile([P, hi - lo], F32, tag="acc")
-                product(acc[:], w1, t, x_code[:, lo:hi], x_scale[:, lo:hi])
-                nc.scalar.activation(out=size[:, lo:hi], in_=acc[:], func=ACT.Abs)
-                nc.scalar.activation(out=root[:, lo:hi], in_=size[:, lo:hi], func=ACT.Abs_reciprocal_sqrt, bias=half)
-                accs.append(acc)
-            if t in SCALAR_SQUARES:
-                nc.scalar.activation(out=scaled[t][:], in_=accs[0][:], func=ACT.Copy, scale=gain[:, t : t + 1])
-                nc.scalar.activation(out=factor[t][:], in_=root[:], func=ACT.Square)
-                held.append((t, accs[0]))
+            root = y_wide[t][:, S:]
+            if t < SPLIT_PLANES:
+                spans, accs = HALVES, [first_halves[t], inverse_root(t, *HALVES[1])]
             else:
+                spans, accs = ((0, S),), [inverse_root(t, 0, S)]
+            if t >= SCALAR_SQUARES_FROM:
+                nc.scalar.activation(out=partner[t][:], in_=accs[0][:], func=ACT.Copy, scale=gain[:, t : t + 1])
+                nc.scalar.activation(out=factor[t][:], in_=root, func=ACT.Square)
+                y_left_in_psum.append((t, accs[0]))
+            else:
+                fetch = nc.vector.tensor_copy if t == 0 else nc.scalar.copy
                 for (lo, hi), acc in zip(spans, accs):
-                    nc.scalar.copy(out=y[t][:, lo:hi], in_=acc[:])
+                    fetch(out=y[t][:, lo:hi], in_=acc[:])
                 nc.vector.scalar_tensor_tensor(
-                    out=factor[t][:], in0=root[:], scalar=gain[:, t : t + 1], in1=root[:], op0=ALU.mult, op1=ALU.mult
+                    out=factor[t][:], in0=root, scalar=gain[:, t : t + 1], in1=root, op0=ALU.mult, op1=ALU.mult
                 )
-            if t in (1, 2):
+            if 0 < t < LAST:
                 normalise(t - 1, 1)
             normalise(t, 0)
-        normalise(2, 1)
-        normalise(3, 1)
+        normalise(LAST - 1, 1)
+        normalise(LAST, 1)
 
-        z_code = keep.tile([P, S], U32, align_bytes=64)
+        z_code = []
         z_scale = keep.tile([P, S], U8, align_bytes=64)
         for c, (lo, hi) in enumerate(HALVES):
-            packed = raw.tile([P, PACK * (hi - lo)], BF16, tag=f"z_packed{c}", align_bytes=64)
-            interleave(nc.scalar.copy if c == 0 else nc.vector.tensor_copy, packed[:], z[c][:])
-            nc.vector.quantize_mx(out=z_code[:, lo:hi].bitcast(FP8X4), scales=z_scale[:, lo:hi], in_=packed[:])
-        for t, acc in held:
-            nc.scalar.copy(out=y[t][:], in_=acc[:])
+            z_packed = reuse.tile([P, PACK * (hi - lo)], BF16, tag=f"z_packed{c}", align_bytes=64)
+            interleave(nc.scalar.copy if c == 0 else nc.vector.tensor_copy, z_packed[:], z[c][:])
+            code_tag = "z_code0" if c == 0 else "z_packed0"
+            z_code.append(reuse.tile([P, hi - lo], U32, name=f"z_code{c}", tag=code_tag, align_bytes=64))
+            nc.vector.quantize_mx(out=z_code[c][:].bitcast(FP8X4), scales=z_scale[:, lo:hi], in_=z_packed[:])
         for t in range(PACK):
-            for lo, hi in HALVES:
+            for c, (lo, hi) in enumerate(HALVES):
                 acc = psum.tile([P, hi - lo], F32, tag="acc")
-                product(acc[:], w2, t, z_code[:, lo:hi], z_scale[:, lo:hi])
+                product(acc[:], w2, t, z_code[c][:], z_scale[:, lo:hi])
                 nc.scalar.copy(out=h_wide[t][:, lo:hi], in_=acc[:])
                 nc.scalar.copy(out=h[t][:, lo:hi], in_=acc[:])
+            if t == 0:
+                for u, y_acc in y_left_in_psum:
+                    nc.scalar.copy(out=y[u], in_=y_acc[:])
 
-        spans = ((0, BULK), (BULK, S))
-        y_far = [raw.tile([P, S], F32, name=f"y_far{t}", tag=f"z_packed{1 - t}", align_bytes=64) for t in range(EARLY_TILES)]
-        for t in range(EARLY_TILES):
-            for lo, hi in spans:
-                nc.vector.tensor_copy(out=y_far[t][:, lo:hi], in_=y[t][:].indirect(entries(n4_sb, lo, hi)))
+        y_far0 = reuse.tile([P, S], F32, tag="z_packed1", align_bytes=64)
+        nc.vector.tensor_copy(out=y_far0[:], in_=y_wide[0][:].indirect(n4_sb[:]))
 
         out_code = keep.tile([P, S], U32, align_bytes=64)
         out_scale = keep.tile([P, S], U8, align_bytes=64)
@@ -199,51 +218,63 @@ def tile_picked_skipflowbnorm_none_po_kernel(
             nc.vector.scalar_tensor_tensor(
                 out=near, in0=y[t][:, lo:hi], scalar=near_gain, in1=step2[:], op0=ALU.mult, op1=ALU.mult
             )
-            if t < EARLY_TILES:
-                nc.vector.tensor_tensor(far, y_far[t][:, lo:hi], step3[:], ALU.mult)
+            if t == 0:
+                nc.vector.tensor_tensor(far, y_far0[:, lo:hi], step3[:], ALU.mult)
             else:
-                nc.vector.tensor_tensor(far, y[t][:].indirect(entries(n4_sb, lo, hi)), step3[:], ALU.mult)
+                nc.vector.tensor_tensor(far, y_wide[t][:].indirect(entries(n4_sb, lo, hi)), step3[:], ALU.mult)
 
-        def hand_on(copy, res, lo, hi, first):
-            packed = keep.tile([P, PACK * (hi - lo)], BF16, name=f"out_packed{lo}", align_bytes=64)
-            interleave(copy, packed[:], res[:, :, lo - first : hi - first])
-            nc.vector.quantize_mx(out=out_code[:, lo:hi].bitcast(FP8X4), scales=out_scale[:, lo:hi], in_=packed[:])
-
-        bulk = keep.tile([P, PACK, BULK], F32)
-        for t in range(PACK):
-            near = work.tile([P, BULK], F32)
-            far = work.tile([P, BULK], F32)
-            terms(t, 0, BULK, h_wide[t], h[t], near[:], far[:], 2.0)
-            turned = psum.tile([P, BULK], F32, tag="acc")
-            for b in range(0, BULK, P):
+        res = [keep.tile([P, PACK, hi - lo], F32, name=f"res{lo}") for lo, hi in PARTS]
+        for t in range(LAST):
+            near_twice = work.tile([P, S], F32, tag="near")
+            far_whole = work.tile([P, S], F32, tag="far")
+            terms(t, 0, S, h_wide[t], h[t], near_twice[:], far_whole[:], 2.0)
+            turned = psum.tile([P, S], F32, tag="acc")
+            for b in range(0, S, P):
+                block = slice(b, b + P)
                 nc.tensor.matmul(
-                    turned[:, b : b + P], near[:, b : b + P], identity[:], start=True, stop=False, is_transpose=True
+                    turned[:, block], near_twice[:, block], identity[:], start=True, stop=False, is_transpose=True
                 )
                 nc.tensor.matmul(
-                    turned[:, b : b + P], far[:, b : b + P], identity[:], start=False, stop=True, is_transpose=True
+                    turned[:, block], far_whole[:, block], identity[:], start=False, stop=True, is_transpose=True
                 )
-            summed = work.tile([P, BULK], F32)
+            summed = work.tile([P, S], F32)
             nc.scalar.activation(out=summed[:], in_=turned[:], func=ACT.Copy, scale=0.5)
-            back = psum.tile([P, BULK], F32, tag="acc")
-            for b in range(0, BULK, P):
+            back = psum.tile([P, S], F32, tag="acc")
+            for b in range(0, S, P):
                 nc.tensor.transpose(back[:, b : b + P], summed[:, b : b + P], identity[:])
-            nc.scalar.copy(out=bulk[:, t, :], in_=back[:])
-            nc.sync.dma_start(out=out_rows[:, t, 0:BULK], in_=bulk[:, t, :])
+            for (lo, hi), part in zip(PARTS, res):
+                nc.scalar.copy(out=part[:, t, :], in_=back[:, lo:hi])
+                nc.sync.dma_start(out=out_rows[:, t, lo:hi], in_=part[:, t, :])
 
-        near_rest = keep.tile([P, PACK, S - BULK], F32)
-        far_rest = keep.tile([P, PACK, S - BULK], F32)
-        for t in range(PACK):
-            terms(t, BULK, S, h[t], h_wide[t], near_rest[:, t, :], far_rest[:, t, :], 1.0)
-        rest = keep.tile([P, PACK, S - BULK], F32)
-        nc.vector.scalar_tensor_tensor(
-            out=rest[:], in0=far_rest[:], scalar=0.5, in1=near_rest[:], op0=ALU.mult, op1=ALU.add
-        )
-        nc.sync.dma_start(out=out_rows[:, :, BULK:S], in_=rest[:])
-        hand_on(nc.scalar.copy, bulk, 0, 256, 0)
-        hand_on(nc.scalar.copy, bulk, 256, BULK, 0)
-        nc.sync.dma_start(out=out_words[:, 0:BULK], in_=out_code[:, 0:BULK].bitcast(I32))
-        hand_on(nc.vector.tensor_copy, rest, BULK, S, BULK)
-        nc.sync.dma_start(out=out_words[:, BULK:S], in_=out_code[:, BULK:S].bitcast(I32))
+        out_packed = keep.tile([P, PACK * S], BF16, align_bytes=64)
+
+        def add_up(c, near, far):
+            lo, hi = PARTS[c]
+            nc.vector.scalar_tensor_tensor(
+                out=res[c][:, LAST, :], in0=far[:], scalar=0.5, in1=near[:], op0=ALU.mult, op1=ALU.add
+            )
+            nc.sync.dma_start(out=out_rows[:, LAST, lo:hi], in_=res[c][:, LAST, :])
+
+        def quantise(lo, hi):
+            nc.vector.quantize_mx(
+                out=out_code[:, lo:hi].bitcast(FP8X4),
+                scales=out_scale[:, lo:hi],
+                in_=out_packed[:, PACK * lo : PACK * hi],
+            )
+
+        near_part = [work.tile([P, hi - lo], F32, name="near_part", tag="near") for lo, hi in PARTS]
+        far_part = [work.tile([P, hi - lo], F32, name="far_part", tag="far") for lo, hi in PARTS]
+        terms(LAST, 0, BULK, h_wide[LAST], h[LAST], near_part[0][:], far_part[0][:], 1.0)
+        add_up(0, near_part[0], far_part[0])
+        interleave(nc.scalar.copy, out_packed[:, 0 : PACK * HALF], res[0][:, :, 0:HALF])
+        interleave(nc.scalar.copy, out_packed[:, PACK * HALF : PACK * BULK], res[0][:, :, HALF:BULK])
+        terms(LAST, BULK, S, h[LAST], h_wide[LAST], near_part[1][:], far_part[1][:], 1.0)
+        quantise(0, HALF)
+        add_up(1, near_part[1], far_part[1])
+        interleave(nc.vector.tensor_copy, out_packed[:, PACK * BULK :], res[1][:])
+        nc.sync.dma_start(out=out_words[:, 0:HALF], in_=out_code[:, 0:HALF].bitcast(I32))
+        quantise(HALF, S)
+        nc.sync.dma_start(out=out_words[:, HALF:S], in_=out_code[:, HALF:S].bitcast(I32))
         for q in range(4):
             queue = nc.scalar if q % 2 == 0 else nc.sync
             queue.dma_start(

from contextlib import ExitStack

import concourse.mybir as mybir
from concourse.masks import make_identity

F32 = mybir.dt.float32
BF16 = mybir.dt.bfloat16
I32 = mybir.dt.int32
U32 = mybir.dt.uint32
U16 = mybir.dt.uint16
U8 = mybir.dt.uint8
FP8X4 = mybir.dt.float8_e4m3fn_x4
FP4X4 = mybir.dt.float4_e2m1fn_x4
ALU = mybir.AluOpType
ACT = mybir.ActivationFunctionType

P = 128
PACK = 4
T = 2048
S = 512
W = 512
PER_COLUMN = 16
FLOPS = 2 * 2 * 512 * 512 * 512

HALF = S // 2
HALVES = ((0, HALF), (HALF, S))
BULK = 384
PARTS = ((0, BULK), (BULK, S))
SPLIT_PLANES = 2
SCALAR_SQUARES_FROM = 2
LAST = PACK - 1


def load_scale_rows(queues, scale_tile, rows):
    for q, queue in enumerate(queues):
        queue.dma_start(
            out=scale_tile[32 * q : 32 * q + 4, :].bitcast(I32), in_=rows[4 * q : 4 * q + 4, :].bitcast(I32)
        )


def interleave(copy, packed, planes):
    copy(
        out=packed.rearrange("p (c i t) -> p c t i", i=4, t=PACK),
        in_=planes.rearrange("p t (c i) -> p c t i", i=4),
    )


def entries(list_tile, lo, hi):
    return list_tile[:, lo // PER_COLUMN : hi // PER_COLUMN]


def tile_picked_skipflowbnorm_none_po_kernel(
    tc, x_words, x_scales, w1_words, w1_scales, gn, w2_words, w2_scales, offs, n1, n2, n3, n4, out_0, out_1, out_2
):
    nc = tc.nc
    with ExitStack() as ctx:
        lists = ctx.enter_context(tc.tile_pool(name="lists", bufs=1))
        keep = ctx.enter_context(tc.tile_pool(name="keep", bufs=1))
        reuse = ctx.enter_context(tc.tile_pool(name="reuse", bufs=1))
        work = ctx.enter_context(tc.tile_pool(name="work", bufs=3))
        psum = ctx.enter_context(tc.psum_pool(name="psum", bufs=8))

        consts = keep.tile([P, 16], F32)
        nc.gpsimd.memset(consts[:], 0.5)
        one_half = consts[:, 8:9]
        gain = consts[:, 0:PACK]
        table_warm = keep.tile([P, 1], F32)
        nc.scalar.activation(out=table_warm[:], in_=one_half, func=ACT.Abs_reciprocal_sqrt, bias=one_half)
        w1_scale_raw = reuse.tile([P, W], U8, tag="w1_scale_raw", align_bytes=64)
        nc.gpsimd.memset(w1_scale_raw[:].bitcast(I32), 0)
        x_scale_table = keep.tile([P, T], U8, align_bytes=64)
        nc.vector.memset(x_scale_table[:].bitcast(I32), 0)
        w2_scale_raw = reuse.tile([P, W], U8, tag="w2_scale_raw")
        nc.vector.memset(w2_scale_raw[:].bitcast(I32), 0)

        offs_sb = lists.tile([P, S // PER_COLUMN], U16)
        nc.sync.dma_start(offs_sb[:], offs)
        w1_raw = reuse.tile([P, 2 * W], U8, tag="w_raw")
        nc.scalar.dma_start(out=w1_raw[:].bitcast(I32), in_=w1_words[0].bitcast(I32))
        x_word_table = keep.tile([P, T], U32, align_bytes=64)
        nc.sync.dma_start(
            out=x_word_table[:].bitcast(I32), in_=x_words[0].rearrange("p c r -> p (c r)").bitcast(I32)
        )
        load_scale_rows([nc.scalar] * 4, x_scale_table, x_scales[0])
        load_scale_rows([nc.scalar] * 2 + [nc.gpsimd] * 2, w1_scale_raw, w1_scales[0])
        nc.gpsimd.dma_start(out=gain, in_=gn.rearrange("(p t) o -> p (t o)", t=PACK))

        def regroup(words_raw, scales_raw, name, words_tag, scale_engine):
            words = reuse.tile([P, 2 * W], U8, name=name + "_words", tag=words_tag, align_bytes=64)
            scales = keep.tile([P, W], U8, name=name + "_scales", align_bytes=64)
            nc.vector.tensor_copy(
                out=words[:].bitcast(U16).rearrange("p (t m) -> p t m", t=PACK),
                in_=words_raw[:].bitcast(U16).rearrange("p (m t) -> p t m", t=PACK),
            )
            scale_engine.tensor_copy(
                out=scales[:].rearrange("p (t m) -> p t m", t=PACK),
                in_=scales_raw[:].rearrange("p (m t) -> p t m", t=PACK),
            )
            return words, scales

        def product(acc, weights, t, codes, scales):
            words, weight_scales = weights
            nc.tensor.matmul_mx(
                out=acc,
                lhsT=words[:, 2 * P * t : 2 * P * (t + 1)].bitcast(FP4X4),
                lhsT_scale=weight_scales[:, P * t : P * (t + 1)],
                rhs=codes.bitcast(FP8X4),
                rhs_scale=scales,
                start=True,
                stop=True,
            )

        w1 = regroup(w1_raw, w1_scale_raw, "w1", "w1_words", nc.vector)
        x_scale = keep.tile([P, S], U8, align_bytes=64)
        x_code = keep.tile([P, S], U32, align_bytes=64)
        for lo, hi in HALVES:
            nc.vector.tensor_copy(out=x_scale[:, lo:hi], in_=x_scale_table[:].indirect(entries(offs_sb, lo, hi)))
            nc.vector.tensor_copy(out=x_code[:, lo:hi], in_=x_word_table[:].indirect(entries(offs_sb, lo, hi)))

        n1_sb = lists.tile([P, S // PER_COLUMN], U16)
        nc.sync.dma_start(n1_sb[:], n1)
        load_scale_rows([nc.scalar] * 4, w2_scale_raw, w2_scales[0])
        w2_raw = reuse.tile([P, 2 * W], U8, tag="w_raw")
        nc.scalar.dma_start(out=w2_raw[:].bitcast(I32), in_=w2_words[0].bitcast(I32))
        n4_sb = lists.tile([P, S // PER_COLUMN], U16)
        nc.sync.dma_start(n4_sb[:], n4)
        n2_sb = lists.tile([P, S // PER_COLUMN], U16)
        nc.sync.dma_start(n2_sb[:], n2)
        n3_sb = lists.tile([P, S // PER_COLUMN], U16)
        nc.sync.dma_start(n3_sb[:], n3)
        w2 = regroup(w2_raw, w2_scale_raw, "w2", "w1_scale_raw", nc.gpsimd)

        identity = keep.tile([P, P], F32)
        make_identity(nc, identity[:])

        y_wide = [keep.tile([P, 2 * S], F32, name=f"y_wide{t}") for t in range(PACK)]
        y = [wide[:, 0:S] for wide in y_wide]
        z = [keep.tile([P, PACK, hi - lo], F32, name=f"z{lo}") for lo, hi in HALVES]
        h_wide = [keep.tile([P, 2 * S], F32, name=f"h_wide{t}") for t in range(PACK)]
        h = [keep.tile([P, S], F32, name=f"h{t}") for t in range(PACK)]
        factor = [keep.tile([P, S], F32, name=f"factor{t}") for t in range(PACK)]
        partner = [
            keep.tile([P, S], F32, name=f"gained_y{t}") if t >= SCALAR_SQUARES_FROM else y[t] for t in range(PACK)
        ]
        y_left_in_psum = []

        def normalise(t, c):
            lo, hi = HALVES[c]
            nc.vector.tensor_tensor(
                z[c][:, t, :], factor[t][:].indirect(entries(n1_sb, lo, hi)), partner[t][:, lo:hi], ALU.mult
            )

        def inverse_root(t, lo, hi):
            acc = psum.tile([P, hi - lo], F32, tag="acc")
            product(acc[:], w1, t, x_code[:, lo:hi], x_scale[:, lo:hi])
            size = h_wide[t][:, S + lo : S + hi]
            nc.scalar.activation(out=size, in_=acc[:], func=ACT.Abs)
            nc.scalar.activation(
                out=y_wide[t][:, S + lo : S + hi], in_=size, func=ACT.Abs_reciprocal_sqrt, bias=one_half
            )
            return acc

        first_halves = [inverse_root(t, *HALVES[0]) for t in range(SPLIT_PLANES)]
        for t in range(PACK):
            root = y_wide[t][:, S:]
            if t < SPLIT_PLANES:
                spans, accs = HALVES, [first_halves[t], inverse_root(t, *HALVES[1])]
            else:
                spans, accs = ((0, S),), [inverse_root(t, 0, S)]
            if t >= SCALAR_SQUARES_FROM:
                nc.scalar.activation(out=partner[t][:], in_=accs[0][:], func=ACT.Copy, scale=gain[:, t : t + 1])
                nc.scalar.activation(out=factor[t][:], in_=root, func=ACT.Square)
                y_left_in_psum.append((t, accs[0]))
            else:
                fetch = nc.vector.tensor_copy if t == 0 else nc.scalar.copy
                for (lo, hi), acc in zip(spans, accs):
                    fetch(out=y[t][:, lo:hi], in_=acc[:])
                nc.vector.scalar_tensor_tensor(
                    out=factor[t][:], in0=root, scalar=gain[:, t : t + 1], in1=root, op0=ALU.mult, op1=ALU.mult
                )
            if 0 < t < LAST:
                normalise(t - 1, 1)
            normalise(t, 0)
        normalise(LAST - 1, 1)
        normalise(LAST, 1)

        z_code = []
        z_scale = keep.tile([P, S], U8, align_bytes=64)
        for c, (lo, hi) in enumerate(HALVES):
            z_packed = reuse.tile([P, PACK * (hi - lo)], BF16, tag=f"z_packed{c}", align_bytes=64)
            interleave(nc.scalar.copy if c == 0 else nc.vector.tensor_copy, z_packed[:], z[c][:])
            code_tag = "z_code0" if c == 0 else "z_packed0"
            z_code.append(reuse.tile([P, hi - lo], U32, name=f"z_code{c}", tag=code_tag, align_bytes=64))
            nc.vector.quantize_mx(out=z_code[c][:].bitcast(FP8X4), scales=z_scale[:, lo:hi], in_=z_packed[:])
        for t in range(PACK):
            for c, (lo, hi) in enumerate(HALVES):
                acc = psum.tile([P, hi - lo], F32, tag="acc")
                product(acc[:], w2, t, z_code[c][:], z_scale[:, lo:hi])
                nc.scalar.copy(out=h_wide[t][:, lo:hi], in_=acc[:])
                nc.scalar.copy(out=h[t][:, lo:hi], in_=acc[:])
            if t == 0:
                for u, y_acc in y_left_in_psum:
                    nc.scalar.copy(out=y[u], in_=y_acc[:])

        y_far0 = reuse.tile([P, S], F32, tag="z_packed1", align_bytes=64)
        nc.vector.tensor_copy(out=y_far0[:], in_=y_wide[0][:].indirect(n4_sb[:]))

        out_code = keep.tile([P, S], U32, align_bytes=64)
        out_scale = keep.tile([P, S], U8, align_bytes=64)
        out_rows = out_0.rearrange("(p t) j -> p t j", t=PACK)
        out_words = out_1[0].rearrange("p c r -> p (c r)").bitcast(I32)

        def terms(t, lo, hi, window, here, near, far, near_gain):
            step2 = work.tile([P, hi - lo], F32)
            nc.vector.tensor_tensor(step2[:], window[:].indirect(entries(n2_sb, lo, hi)), here[:, lo:hi], ALU.subtract)
            step3 = work.tile([P, hi - lo], F32)
            nc.vector.tensor_tensor(step3[:], window[:].indirect(entries(n3_sb, lo, hi)), here[:, lo:hi], ALU.subtract)
            nc.vector.scalar_tensor_tensor(
                out=near, in0=y[t][:, lo:hi], scalar=near_gain, in1=step2[:], op0=ALU.mult, op1=ALU.mult
            )
            if t == 0:
                nc.vector.tensor_tensor(far, y_far0[:, lo:hi], step3[:], ALU.mult)
            else:
                nc.vector.tensor_tensor(far, y_wide[t][:].indirect(entries(n4_sb, lo, hi)), step3[:], ALU.mult)

        res = [keep.tile([P, PACK, hi - lo], F32, name=f"res{lo}") for lo, hi in PARTS]
        for t in range(LAST):
            near_twice = work.tile([P, S], F32, tag="near")
            far_whole = work.tile([P, S], F32, tag="far")
            terms(t, 0, S, h_wide[t], h[t], near_twice[:], far_whole[:], 2.0)
            turned = psum.tile([P, S], F32, tag="acc")
            for b in range(0, S, P):
                block = slice(b, b + P)
                nc.tensor.matmul(
                    turned[:, block], near_twice[:, block], identity[:], start=True, stop=False, is_transpose=True
                )
                nc.tensor.matmul(
                    turned[:, block], far_whole[:, block], identity[:], start=False, stop=True, is_transpose=True
                )
            summed = work.tile([P, S], F32)
            nc.scalar.activation(out=summed[:], in_=turned[:], func=ACT.Copy, scale=0.5)
            back = psum.tile([P, S], F32, tag="acc")
            for b in range(0, S, P):
                nc.tensor.transpose(back[:, b : b + P], summed[:, b : b + P], identity[:])
            for (lo, hi), part in zip(PARTS, res):
                nc.scalar.copy(out=part[:, t, :], in_=back[:, lo:hi])
                nc.sync.dma_start(out=out_rows[:, t, lo:hi], in_=part[:, t, :])

        out_packed = keep.tile([P, PACK * S], BF16, align_bytes=64)

        def add_up(c, near, far):
            lo, hi = PARTS[c]
            nc.vector.scalar_tensor_tensor(
                out=res[c][:, LAST, :], in0=far[:], scalar=0.5, in1=near[:], op0=ALU.mult, op1=ALU.add
            )
            nc.sync.dma_start(out=out_rows[:, LAST, lo:hi], in_=res[c][:, LAST, :])

        def quantise(lo, hi):
            nc.vector.quantize_mx(
                out=out_code[:, lo:hi].bitcast(FP8X4),
                scales=out_scale[:, lo:hi],
                in_=out_packed[:, PACK * lo : PACK * hi],
            )

        near_part = [work.tile([P, hi - lo], F32, name="near_part", tag="near") for lo, hi in PARTS]
        far_part = [work.tile([P, hi - lo], F32, name="far_part", tag="far") for lo, hi in PARTS]
        terms(LAST, 0, BULK, h_wide[LAST], h[LAST], near_part[0][:], far_part[0][:], 1.0)
        add_up(0, near_part[0], far_part[0])
        interleave(nc.scalar.copy, out_packed[:, 0 : PACK * HALF], res[0][:, :, 0:HALF])
        interleave(nc.scalar.copy, out_packed[:, PACK * HALF : PACK * BULK], res[0][:, :, HALF:BULK])
        terms(LAST, BULK, S, h[LAST], h_wide[LAST], near_part[1][:], far_part[1][:], 1.0)
        quantise(0, HALF)
        add_up(1, near_part[1], far_part[1])
        interleave(nc.vector.tensor_copy, out_packed[:, PACK * BULK :], res[1][:])
        nc.sync.dma_start(out=out_words[:, 0:HALF], in_=out_code[:, 0:HALF].bitcast(I32))
        quantise(HALF, S)
        nc.sync.dma_start(out=out_words[:, HALF:S], in_=out_code[:, HALF:S].bitcast(I32))
        for q in range(4):
            queue = nc.scalar if q % 2 == 0 else nc.sync
            queue.dma_start(
                out=out_2[0][4 * q : 4 * q + 4, :].bitcast(I32), in_=out_scale[32 * q : 32 * q + 4, :].bitcast(I32)
            )
